import numpy as np, ml_dtypes
CORES = [13,21,141,149]
N = 4
BF = ml_dtypes.bfloat16
def gentries(a):
    return np.ascontiguousarray(a.reshape(8, 16, -1).transpose(0, 2, 1)).reshape(8, -1)
def gtable(e):
    e = np.asarray(e); return np.ascontiguousarray(e.reshape(8, -1, 16).transpose(0, 2, 1)).reshape(128, -1).astype(np.int32)
V, H, I, L, R, CAP, MV, RO = 1792, 512, 128, 1024, 512, 96, 4, 2
Z = V + I * RO
W = Z + I * (RO - 1)
def grow(rng, few=0):
    S = H // 8; n = (V - H) // S
    lo = 0.1 + 0.25 * rng.random((N, 8, 1, S)); wd = 0.2 + 0.4 * rng.random((N, 8, 1, S)); sh = 1.5 * rng.standard_normal((N, 8, 16, S))
    def keys(pos):
        x = 15 * (lo[..., None] + wd[..., None] * pos) + sh[..., None] + 0.7 * rng.standard_normal((N, 8, 16, S, 8 + n), dtype=np.float32)
        x = np.clip(np.rint(x), 0, 15).astype(np.int64)
        return np.concatenate([x[..., :8].reshape(N, 8, 16, H), x[..., 8:].reshape(N, 8, 16, V - H)], axis=3)
    half = np.linspace(0.0, 1.0, 2 * n + 1)
    pa = np.concatenate([np.array([0.5, 0.25, 0.75, 0.1, 0.3, 0.5, 0.7, 0.9]), half[1::2]])
    pb = np.concatenate([np.array([1.0, 0.5, 1.0, 0.2, 0.4, 0.6, 0.8, 1.0]), half[2::2]])
    ids = np.concatenate([8 * np.arange(S)[:, None] + np.arange(8), H + n * np.arange(S)[:, None] + np.arange(n)], axis=1)
    kids = [[1, 3, 5] + [8 + 2 * i * n // 10 for i in range(5)], [2, 4, 6] + [8 + (2 * i + 1) * n // 10 for i in range(5)]]
    lk = [np.concatenate([ids[:, k].reshape(-1), np.zeros(V - H, np.int64)]) for k in kids]
    r = np.array([-1, 2, -1, 4, 5, 6, 7, -1] + list(range(9, 8 + n)) + [-1])
    lr = np.where(r >= 0, ids[:, r], -1); lr = np.concatenate([lr[:, :8].reshape(-1), lr[:, 8:].reshape(-1)])
    ph = np.concatenate([np.argsort(rng.random((N, 8, H)), axis=-1), H + np.argsort(rng.random((N, 8, V - H)), axis=-1)], axis=2); inv = np.argsort(ph, axis=-1)
    ka = np.take_along_axis(keys(pa), inv[:, :, None, :], 3); kb = np.take_along_axis(keys(pb), inv[:, :, None, :], 3)
    ca, cb = [np.where(np.arange(V) < H, np.take_along_axis(ph, k[inv], 2), rng.integers(0, R, (N, 8, V))) for k in lk]
    rr = lr[inv]; rt = np.where((rr >= 0) & (rng.random((N, 8, V)) < 0.94), np.take_along_axis(ph, np.maximum(rr, 0), 2), -1)
    it = np.where(rng.random((N, 8, 1, R)) < 0.5, rng.integers(0, 3, (N, 8, 16, R)), rng.integers(0, 16, (N, 8, 16, R)))
    if few:
        pool = 8 * rng.integers(0, S, (N, 8, few)) + rng.integers(3, 8, (N, 8, few)); s = np.take_along_axis(pool, rng.integers(0, few, (N, 8, L)), 2)
    else: s = rng.integers(0, H, (N, 8, L))
    g = s >> 3; top = rng.choice(np.array([1.05, 1.2, 1.5, 2.0]), (N, 8, 1)); top[0, 0] = 2.0; top[1, 0] = 1.05
    u = (top + 0.1) * rng.random((N, 8, L)) - 0.1
    x = 15 * (np.take_along_axis(lo[:, :, 0], g, 2) + np.take_along_axis(wd[:, :, 0], g, 2) * u)
    q = np.clip(np.rint(x[:, :, None] + np.take_along_axis(sh, g[:, :, None, :], 3) + 0.7 * rng.standard_normal((N, 8, 16, L), dtype=np.float32)), 0, 15).astype(np.int64)
    v = np.take_along_axis(ph, s, 2); w = rng.integers(0, 1024, (N, 8, 16))
    return ka, kb, ca, cb, rt, it, q, v, w
def pack(ka, kb, ca, cb, rt, it, q, v, w):
    return {"kk": (ka + 16 * kb).reshape(N, 128, V).astype(np.float32).astype(BF), "c0": ca.astype(np.int32), "c1": cb.astype(np.int32), "rt": rt.astype(np.int32),
            "rec": it.reshape(N, 128, R).astype(np.float32).astype(BF), "qs": q.reshape(N, 128, L).astype(np.float32).astype(BF),
            "v0": np.stack([gtable(a) for a in v]), "wt": w.reshape(N, 128, 1).astype(np.int32)}
def setup_inputs(rng):
    return pack(*grow(rng))
def setup_inputs_room(rng):
    ka, kb, ca, cb, rt, it, q, v, w = grow(rng)
    for a in range(N):
        for g in range(8):
            e = rng.permutation(H)[:8]; z = H + rng.permutation(V - H)[:8]
            ca[a, g, e] = z; cb[a, g, e] = z; rt[a, g, e] = -1; rt[a, g, z] = -1; kb[a, g][:, z] = np.minimum(kb[a, g][:, z], 14)
            n = int(rng.choice(np.array([0, 1, CAP - 1, CAP, CAP + 1, 2 * CAP])))
            if a == 0: n = (CAP, CAP + 1, 2 * CAP, CAP - 1, 1, 0, CAP, CAP + 1)[g]
            if a == 1: n = (CAP, CAP, CAP + 1, 2 * CAP, CAP, CAP, 0, 1)[g]
            o = rng.permutation(L)
            if g % 2 == 0: o = np.concatenate([np.array([0, L - 1]), o[(o > 0) & (o < L - 1)]])
            hot, cool = o[:n], o[n:]
            m = np.argsort(rng.random((16, n)), axis=0); q[a, g][:, hot] = np.where(m < rng.integers(9, 17, n), 15, rng.integers(0, 16, (16, n)))
            m = np.argsort(rng.random((16, L - n)), axis=0); q[a, g][:, cool] = np.where(m < rng.integers(8, 17, L - n), 0, q[a, g][:, cool])
            v[a, g, hot] = rng.choice(e, n)
    return pack(ka, kb, ca, cb, rt, it, q, v, w)
def setup_inputs_crowd(rng):
    ka, kb, ca, cb, rt, it, q, v, w = grow(rng, 6)
    for a in range(N):
        for g in (5, 6, 7):
            if g < 7 or a % 2 == 0:
                z = H + rng.permutation(V - H)[:H + 1]; kb[a, g] = 15; rt[a, g] = -1; ca[a, g, :H] = z[:H]; cb[a, g, :H] = z[:H]
            if g == 5: v[a, g, :I] = rng.permutation(H)[:I]
            if g == 6: v[a, g] = int(rng.integers(0, H))
            if g == 7 and a % 2 == 0:
                e = int(rng.integers(0, H // 4)); y = int(z[H]); ca[a, g, e] = y; cb[a, g, e] = y; kb[a, g, :, y] = rng.integers(0, 14, 16)
                hot = np.concatenate([np.array([0]), 1 + rng.permutation(L - 1)[:CAP - 1]])
                q[a, g][:, hot] = rng.integers(14, 16, (16, CAP)); q[a, g, :, 0] = 15; w[a, g] = 1023
                v[a, g] = rng.integers(H // 4, H, L); v[a, g, hot] = e
            if g == 7 and a % 2 == 1:
                o = rng.permutation(H)[:MV + 2]; y = int(rng.integers(H, V)); kb[a, g][:, o] = 0; kb[a, g, :, y] = 0
                rt[a, g, o[:-1]] = o[1:]; rt[a, g, o[-1]] = -1; rt[a, g, y] = -1; ca[a, g, o[-1]] = y; cb[a, g, o[-1]] = y
                v[a, g] = int(o[0]); q[a, g] = rng.integers(1, 16, (16, L))
    return pack(ka, kb, ca, cb, rt, it, q, v, w)
def setup_inputs_votes(rng):
    ka, kb, ca, cb, rt, it, q, v, w = grow(rng)
    base = rng.integers(2, 12, (N, 8, 16, 1)); kb = base + rng.integers(0, 2, (N, 8, 1, V)); ka = base - rng.integers(0, 2, (N, 8, 1, V))
    m = np.argsort(rng.random((N, 8, 16, L)), axis=2) < rng.choice(np.array([8, 9]), (N, 8, 1, L))
    q = np.where(m, base + 1 + rng.integers(0, 2, (N, 8, 1, L)), base - rng.integers(0, 2, (N, 8, 16, L)))
    it[..., ::2] = 0
    return pack(ka, kb, ca, cb, rt, it, q, v, w)
def setup_inputs_ends(rng):
    ka, kb, ca, cb, rt, it, q, v, w = grow(rng); inner = np.arange(V) < H
    for a in range(N):
        for g in range(8):
            if g % 4 == 0: rt[a, g] = -1
            if g % 4 == 1:
                o = rng.permutation(H); rt[a, g, o] = np.roll(o, -1); o = H + rng.permutation(V - H); rt[a, g, o] = np.roll(o, -1)
            if g % 4 == 2:
                e = np.array([0, H - 1, H, V - 1]); z = np.array([0, R - 1])
                ca[a, g] = np.where(inner, rng.choice(e, V), rng.choice(z, V)); cb[a, g] = np.where(inner, rng.choice(e, V), rng.choice(z, V))
            if g % 4 == 3: rt[a, g] = np.where(rng.random(V) < 0.3, np.arange(V), rt[a, g])
    v[:, :, 0] = 0; v[:, :, L - 1] = H - 1
    return pack(ka, kb, ca, cb, rt, it, q, v, w)
def setup_inputs_spread(rng):
    inner = np.arange(V) < H
    def some(n):
        return np.minimum((16 * rng.random((N, 8, 16, n)) ** rng.choice(np.array([0.4, 1.0, 2.0, 4.0]), (N, 8, 1, n))).astype(np.int64), 15)
    ka, kb, q, it = some(V), some(V), some(L), some(R)
    ca = np.where(inner, rng.integers(0, V, (N, 8, V)), rng.integers(0, R, (N, 8, V))); cb = np.where(inner, rng.integers(0, V, (N, 8, V)), rng.integers(0, R, (N, 8, V)))
    rt = np.where(inner, rng.integers(0, H, (N, 8, V)), rng.integers(H, V, (N, 8, V))); rt = np.where(rng.random((N, 8, V)) < rng.choice(np.array([0.05, 0.2, 0.5]), (N, 8, 1)), -1, rt)
    v = rng.integers(0, H, (N, 8, L))
    for a in range(N):
        for g in range(8):
            o = 1 + rng.permutation(H - 1)[:2]; e = int(o[0]); u = 0 if g % 2 == 0 else int(o[1])
            o = H + rng.permutation(V - H)[:2]; z = int(o[0]); y = int(o[1])
            v[a, g, 0] = e; v[a, g, 1] = u; q[a, g, :, :2] = 0
            kb[a, g, :, e] = 0; ka[a, g, :, z] = np.maximum(ka[a, g, :, z], 1); rt[a, g, e] = u; ca[a, g, e] = z; cb[a, g, e] = z
            ka[a, g, :, u] = 0; kb[a, g, :, u] = 15; ka[a, g, :, y] = 0; ca[a, g, u] = y; cb[a, g, u] = z
    return pack(ka, kb, ca, cb, rt, it, q, v, rng.integers(0, 1024, (N, 8, 16)))
def check_inputs(d):
    bad = []
    for k, hi in (("kk", 255), ("rec", 15), ("qs", 15), ("v0", H - 1), ("wt", 1023)):
        x = np.asarray(d[k]).astype(np.float64)
        if not np.all((x >= 0) & (x <= hi) & (x == np.floor(x))): bad.append("range of " + k)
    for k in ("c0", "c1"):
        x = np.asarray(d[k]).astype(np.int64)
        if not (np.all((x[..., :H] >= 0) & (x[..., :H] < V)) and np.all((x[..., H:] >= 0) & (x[..., H:] < R))): bad.append("range of " + k)
    x = np.asarray(d["rt"]).astype(np.int64); y = x[..., H:]
    if not (np.all((x[..., :H] >= -1) & (x[..., :H] < H)) and np.all((y == -1) | ((y >= H) & (y < V)))): bad.append("range of rt")
    return bad
def above(a, b):
    return np.sum(a > b, axis=2) >= 9
def pick(t, ix):
    return np.take_along_axis(t, ix[:, :, None, :] if t.ndim == 4 else ix, -1)
def lowest(ok, u):
    i = np.arange(u.shape[2]); key = np.where(ok, u, W + i)
    return ok & ~np.any((key[..., :, None] == key[..., None, :]) & (i[None, :] < i[:, None]), axis=3)
def insert(ka, kb, ca, cb, gr, win, n, m, p, cn, new):
    a, e, i = np.nonzero(win); n = n[a, e, i]; m = m[a, e, :, i]; p = p[a, e, i]; cn = cn[a, e, i]; x = new[i]
    k0 = ka[a, e, :, n]; k1 = kb[a, e, :, n]; b = np.sum(m > k0, axis=1) >= 9
    o0 = np.where(b, ca[a, e, n], cn); o1 = np.where(b, cn, cb[a, e, n])
    ka[a, e, :, x] = k1; kb[a, e, :, x] = k1; ca[a, e, x] = o1; cb[a, e, x] = o1; gr[a, e, x] = gr[a, e, n]; gr[a, e, n] = x
    kb[a, e, :, n] = np.where(b[:, None], m, k0); ka[a, e, :, n] = np.where(b[:, None], k0, m)
    cb[a, e, n] = np.where(b, p, o0); ca[a, e, n] = np.where(b, o0, p)
def reference(kk, c0, c1, rt, rec, qs, v0, wt):
    k = kk.astype(np.float32).astype(np.int16).reshape(N, 8, 16, V)
    ka = np.zeros((N, 8, 16, W), np.int16); kb = np.zeros((N, 8, 16, W), np.int16); ka[..., :V] = k & 15; kb[..., :V] = k >> 4
    ca = np.zeros((N, 8, W), np.int64); cb = np.zeros((N, 8, W), np.int64); gr = np.zeros((N, 8, W), np.int64)
    ca[..., :V] = c0; cb[..., :V] = c1; gr[..., :V] = rt
    it = rec.astype(np.float32).astype(np.int16).reshape(N, 8, 16, R); q = qs.astype(np.float32).astype(np.int16).reshape(N, 8, 16, L)
    wg = wt.astype(np.int64).reshape(N, 8, 16); v = np.stack([gentries(a) for a in v0]).astype(np.int64); fi = np.array(v)
    pon = np.zeros((N, 8, I), bool); pv = np.zeros((N, 8, I), np.int64); pf = np.zeros((N, 8, I), np.int64); lane = np.arange(I)
    for t in range(RO):
        for step in range(MV + 1):
            hi = above(q, pick(kb, v)); b = above(q, pick(ka, v)); g = pick(gr, v); c = np.where(b, pick(cb, v), pick(ca, v)); leaf = (v >= H) & (v < Z)
            if step == MV: break
            right = hi & (g >= 0); down = ~right & ~leaf
            fi = np.where(down, v, fi); v = np.where(right, g, np.where(down, c, v))
        done = leaf & ~hi; over = hi & (g < 0)
        if t > 0:
            m = pick(kb, pv); gu = pick(gr, pf); u = np.where(above(m, pick(kb, pf)) & (gu >= 0), gu, pf)
            cu = np.where(above(m, pick(ka, u)), pick(cb, u), pick(ca, u)); ok = pon & (cu == pv)
            insert(ka, kb, ca, cb, gr, lowest(ok, u), u, m, pv, np.broadcast_to(V + I * (t - 1) + lane, pv.shape), Z + I * (t - 1) + lane)
        pv = np.array(v[:, :, :I]); pf = np.array(fi[:, :, :I]); pon = lowest(done[:, :, :I], pv)
        insert(ka, kb, ca, cb, gr, pon, pv, q[..., :I], c[:, :, :I], c[:, :, :I], V + I * t + lane)
        q = np.where(done[:, :, None, :], (q + pick(it, np.where(done, c, 0)) + t) & 15, q).astype(np.int16); v = np.where(done, fi, v)
        before = np.add.accumulate(over.astype(np.int64), axis=2) - over
        a, e, l = np.nonzero(over & (before < CAP)); s = before[a, e, l]
        box = np.zeros((N, 8, 16, CAP), np.int16); have = np.zeros((N, 8, CAP), bool); box[a, e, :, s] = q[a, e, :, l]; have[a, e, s] = True
        src = (a - 1) % N; nq = np.where(have[src, e, s][:, None], box[src, e, :, s], q[a, e, :, l])
        q[a, e, :, l] = nq; st = np.sum(nq.astype(np.int64) * wg[a, e], axis=1) & (H - 1); v[a, e, l] = st; fi[a, e, l] = st
    return {"yk": (ka + 16 * kb).reshape(N, 128, W).astype(np.float32).astype(BF), "y0": ca.astype(np.float32), "y1": cb.astype(np.float32), "yr": gr.astype(np.float32),
            "yq": q.reshape(N, 128, L).astype(np.float32).astype(BF)}

from concourse.mybir import AluOpType as ALU, ActivationFunctionType as AF

BF, F32, I32, U16, F16 = "bfloat16", "float32", "int32", "uint16", "float16"
NMAT = 44
SLACK, LOOK, TOL, MARG, ITER, STEP = 600, 30, 200, 800, 100, 100
TV = 192
NE = 8
SB = {
    "KO": ([128, 2304], BF), "A": ([128, 1920], F32), "P": ([128, 2304], F32), "TT": ([128, 1792], BF),
    "q0": ([128, 1152], BF), "q1": ([128, 1152], BF), "q2": ([128, 1152], BF),
    "Q0": ([128, 1024], F32), "Q1": ([128, 1024], F32), "rc0": ([128, 528], BF), "rc1": ([128, 528], BF),
    "V0": ([128, 64], I32), "OFF": ([128, 640], U16), "R": ([128, 1024], BF), "B": ([128, 1024], BF),
    "PG": ([128, 1024], BF), "PL": ([128, 1024], BF), "X": ([128, 1024], BF), "GE": ([128, 1024], BF),
    "CI": ([128, 128], I32), "CL": ([128, 320], I32), "HI": ([128, 128], I32), "HL": ([128, 320], I32),
    "DI": ([128, 384], BF), "DL": ([128, 960], BF), "WB0": ([128, 272], BF), "WB1": ([128, 272], BF),
    "WS": ([128, 8, 272], BF), "WM": ([128, NMAT, 8, 16], BF), "ZE": ([128, 8, 16], BF), "ON": ([128, 128], BF),
    "IT": ([128, 16], I32), "IT2": ([128, 16], I32), "BO": ([128, 128], BF), "BT": ([128, 128], BF),
    "NB": ([128, 128], BF), "UP": ([128, 128], BF), "US": ([128, 128], BF),
    "RO": ([128, 16], F32), "CO": ([128, 32], F32), "IH": ([128, 4], F32), "I4": ([128, 8], I32),
    "TS": ([128, 128], BF), "SX": ([128, 4, 128], F16), "WPM": ([128, 56], BF), "WPL": ([128, 56], BF),
    "WBB": ([128, 40], BF), "WP": ([128, 144], BF), "WW": ([128, 144], BF), "WT": ([128, 4], I32), "W2": ([128, 4], I32),
    "SW": ([128, 128], F32), "PN": ([128, 16], BF), "LW": ([128, 24], F32), "XH": ([128, 128], BF), "XL": ([128, 128], BF),
    "XC": ([128, 128], BF), "S15": ([128, 3, 128], BF),
    "TH0": ([128, 96], F32), "TH1": ([128, 96], F32), "F0": ([128, 96], BF), "F1": ([128, 96], BF),
    "VT0": ([128, 164, 4], F16), "VT1": ([128, 164, 4], F16), "DN": ([128, 256], BF), "DV": ([128, 256], F32),
    "ND": ([128, 256], F32), "FS": ([128, 256], F32), "FD": ([128, 64], F32), "PX": ([128, 128], U16),
    "OW": ([128, 128], BF), "INC": ([128, 72], F32), "SG": ([128, 8], F32), "JK": ([128, 384], BF), "CU": ([128, 8], U16),
    "CB": ([128, 16], BF), "CM": ([128, 96], BF), "LN": ([128, 16], U16), "SE0": ([128, 192], BF), "SE1": ([128, 192], BF),
    "RB0": ([128, 192], BF), "RB1": ([128, 192], BF), "RX0": ([128, 192], BF), "RX1": ([128, 192], BF),
    "TQ": ([128, 96], BF), "SL": ([128, 128], BF), "VB": ([128, 128], F32), "HS": ([128, 128], I32),
    "kg": ([128, 384], BF), "bb": ([128, 384], BF), "KV": ([128, 8], F32), "ES": ([128, 576], BF),
    "wn": ([128, 128], BF), "NP": ([128, 128], F32), "TG": ([128, 32], U16),
    "vk": ([128, 256], BF), "va": ([128, 256], F32), "vp": ([128, 256], F32), "vq": ([128, 256], F32),
    "mz": ([128, 256], BF), "MQ": ([128, 128], F32), "Re": ([128, 384], BF), "t1": ([128, 128], F32), "PF": ([128, 16], F16),
    "ZE2": ([128, 8], F32), "WH": ([128, 144], F16), "IF": ([128, 128], F16), "LF": ([128, 24], F16), "tf": ([128, 128], F16),
}
SCRATCH = {k: ("sbuf", v[0], v[1]) for k, v in SB.items()}
for _i in range(8):
    SCRATCH["p%d" % _i] = ("psum", [128, 512], F32)
SEMAPHORES = ["sv", "ss", "sp", "sg", "ls", "lr", "ra0", "ra1", "rx0", "rx1"] + ["d%d" % _i for _i in range(32)]
SIZE = {BF: 2, F16: 2, U16: 2, F32: 4, I32: 4}
QC = -3064.5
THN = -49016.0
ALL = slice(None)


def ap(name, *idx):
    return (name, idx)


def sl(a, b, s=None):
    return slice(a, b, s)


def c(name, a, b, s=None):
    return (name, (ALL, slice(a, b, s)))


def ind(win, off):
    return ("@", win, off)


def box(x):
    name, idx = x
    shape = SCRATCH[name][1]
    idx = list(idx) + [ALL] * (len(shape) - len(idx))
    lo, hi, n, stride = 0, 0, 1, 1
    for d in range(len(shape) - 1, 0, -1):
        i = idx[d]
        r = range(shape[d])[i] if isinstance(i, slice) else [i]
        lo += r[0] * stride
        hi += r[-1] * stride
        n *= len(r)
        stride *= shape[d]
    r = range(shape[0])[idx[0]]
    st = 1
    if isinstance(idx[-1], slice) and (idx[-1].step or 1) > 1 and (len(shape) == 2 or shape[-1] % idx[-1].step == 0):
        st = idx[-1].step
    return (name, r[0], r[-1] + 1, lo, hi + 1, st), n


def res(T, x):
    if not isinstance(x, tuple):
        return x
    if x[0] == "@":
        return res(T, x[1]).indirect(res(T, x[2]))
    return T[x[0]][x[1]] if x[1] else T[x[0]][:]


def program():
    ops = []
    prev = {}

    def regs(xs):
        out = []
        for x in xs:
            if isinstance(x, tuple):
                if x[0] == "@":
                    out += [box(x[1])[0], box(x[2])[0]]
                elif x[0] in SCRATCH:
                    out.append(box(x)[0])
        return out

    def add(alts, rd, wr, kind="c", extra=None):
        wr2 = [w[1] if w[0] == "@" else w for w in wr]
        rd2 = list(rd) + [w[2] for w in wr if w[0] == "@"]
        ops.append({"alts": alts, "rd": regs(rd2), "wr": regs(wr2), "kind": kind, "x": extra})

    def nel(x):
        return 16 * box(x[2])[1] if x[0] == "@" else box(x)[1]

    def dty(x):
        return SCRATCH[(x[1] if x[0] == "@" else x)[0]][2]

    def ps(x):
        return x[0] != "@" and SCRATCH[x[0]][0] == "psum"

    def vcost(out, ins, two=False):
        n = nel(ins[0])
        if out[0] == "@":
            return 60 + 3.8 * n
        if ins[0][0] == "@":
            return 60 + 1.56 * n
        if two:
            return 25 + max(64, n * (1 if ps(ins[0]) or ps(ins[1]) else 2))
        return 25 + max(64, n * (0.5 if all(SIZE[dty(x)] == 2 for x in [out] + ins) else 1))

    def tt(out, a, b, op):
        add([("v", vcost(out, [a, b], True), lambda q, T: q.tensor_tensor(res(T, out), res(T, a), res(T, b), op))], [a, b], [out])

    def ts(out, a, s1, s2, op0, op1=None):
        if op1 is None:
            f = lambda q, T: q.tensor_scalar(res(T, out), res(T, a), res(T, s1), None, op0)
        else:
            f = lambda q, T: q.tensor_scalar(res(T, out), res(T, a), res(T, s1), res(T, s2), op0, op1)
        add([("v", vcost(out, [a]), f)], [a, s1, s2], [out])

    def cp(out, a):
        add([("v", vcost(out, [a]), lambda q, T: q.tensor_copy(res(T, out), res(T, a)))], [a], [out])

    def scost(a):
        return (75 + 1.56 * nel(a)) if a[0] == "@" else 40 + max(64, nel(a))

    def act(out, a, fn, bias=0.0, scale=1.0, acc=None):
        if acc is None:
            f = lambda q, T: q.activation(res(T, out), res(T, a), fn, bias=res(T, bias), scale=res(T, scale))
        else:
            f = lambda q, T: q.activation(res(T, out), res(T, a), fn, bias=res(T, bias), scale=res(T, scale), accum_out=res(T, acc))
        add([("s", scost(a) + (20 if acc else 0), f)], [a, bias, scale], [out] + ([acc] if acc else []))

    def aff(out, a, scale=1.0, bias=0.0, eng="vs"):
        alts = []
        if scale == 1.0 and bias == 0.0:
            alts.append(("v", vcost(out, [a]), lambda q, T: q.tensor_copy(res(T, out), res(T, a))))
        else:
            alts.append(("v", vcost(out, [a]), lambda q, T: q.tensor_scalar(res(T, out), res(T, a), res(T, scale), res(T, bias), ALU.mult, ALU.add)))
        if "s" in eng:
            alts.append(("s", scost(a), lambda q, T: q.activation(res(T, out), res(T, a), AF.Identity, bias=res(T, bias), scale=res(T, scale))))
        add(alts, [a, scale, bias], [out])

    def ge(out, a, th, sgn=1.0):
        alts = [("v", vcost(out, [a]), lambda q, T: q.tensor_scalar(res(T, out), res(T, a), th, None, ALU.is_gt if sgn > 0 else ALU.is_lt)),
                ("s", scost(a), lambda q, T: q.activation(res(T, out), res(T, a), AF.Sigmoid, bias=-256.0 * sgn * th, scale=256.0 * sgn))]
        add(alts, [a], [out])

    def fill(out, val):
        if val == int(val):
            iota(out, [[0, nel(out)]], int(val), 0)
        else:
            aff(out, c("ON", 0, nel(out)), 0.0, val)

    def chain(key):
        if key in prev:
            ops[-1]["after"] = prev[key]
        prev[key] = len(ops) - 1

    def ms(out, val):
        add([("v", vcost(out, [out]), lambda q, T: q.memset(res(T, out), val))], [], [out])

    def scan(out, d0, d1):
        add([("v", vcost(out, [d0, d1]), lambda q, T: q.tensor_tensor_scan(res(T, out), res(T, d0), res(T, d1), 0.0, ALU.mult, ALU.add))], [d0, d1], [out])

    def iota(out, pat, base, cm):
        if dty(out) != I32:
            f = lambda q, T: q.iota(res(T, out), pat, base, cm, allow_small_or_imprecise_dtypes=True)
        else:
            f = lambda q, T: q.iota(res(T, out), pat, base, cm)
        add([("g", 140 + 2 * nel(out), f)], [], [out])

    def asel(out, a, pat, op, val, base, cm):
        add([("g", 180 + 2 * nel(out), lambda q, T: q.affine_select(res(T, out), res(T, a), pat, op, float(val), base, cm))], [a], [out])

    def mm(lst, first=True, last=True):
        def f(q, T):
            for k, (o, l, r) in enumerate(lst):
                m = q.matmul(res(T, o), res(T, l), res(T, r), first and k == 0, last and k == len(lst) - 1)
            return m
        cost = sum(0.5 * max(min(64, nel(l)), nel(r)) + 5 for o, l, r in lst)
        add([("p", cost, f)], [x for o, l, r in lst for x in (l, r)], [o for o, l, r in lst])

    nd = [0]

    def dma(eng, out, a, nbytes):
        k = nd[0]
        nd[0] += 1
        add([(eng, 60, lambda q, T: q.dma_start(res(T, out), res(T, a)))], [a], [out], "d", ("d%d" % k, 1900 + nbytes / 180.0))

    dma("y", c("KO", 128, 640), c("kk", 0, 512), 131072)
    for k, nm in enumerate(("c0", "c1", "rt")):
        dma("s" if k == 1 else "y", ap("CI", sl(32 + 32 * k, 64 + 32 * k)), c(nm, 0, 512), 16384)
    dma("s", ap("V0"), ap("v0"), 32768)
    dma("s", c("q0", 0, 512), c("qs", 0, 512), 131072)
    dma("y", c("q0", 512, 1024), c("qs", 512, 1024), 200000)
    for k, nm in enumerate(("c0", "c1", "rt")):
        dma("y", ap("CL", sl(32 + 32 * k, 64 + 32 * k)), c(nm, 512, 1792), 200000)
    dma("y", c("KO", 640, 1920), c("kk", 512, 1792), 500000)
    dma("y", c("rc0", 0, 512), ap("rec"), 600000)
    dma("y", c("WT", 0, 1), ap("wt"), 1000)

    ms(ap("ON"), 1.0)
    ms(ap("ZE"), 0.0)
    ms(c("ZE2", 0, 2), -8.0)
    act(c("F0", 0, 32), c("ON", 0, 32), AF.Sigmoid, scale=256.0)
    fill(c("F1", 0, 32), 1.0)
    iota(ap("IT"), [[-1, 16]], 128, 1)
    chain("g")
    asel(c("TS", 32, 64), c("ON", 0, 32), [[4, 32]], ALU.is_ge, 0.0, 3, -1)
    asel(c("TS", 0, 32), c("TS", 32, 64), [[-4, 32]], ALU.is_ge, 0.0, 0, 1)
    chain("g")
    asel(ap("BT"), ap("ON"), [[-16, 8], [0, 16]], ALU.is_ge, 0.0, 0, 1)
    asel(ap("BO"), ap("BT"), [[16, 8], [0, 16]], ALU.is_ge, 0.0, 15, -1)
    chain("g")
    iota(ap("CI", sl(0, 32)), [[1, 128]], 0, 128)
    chain("g")
    iota(ap("CL", sl(0, 32)), [[1, 320]], 512, 320)
    chain("g")
    M = {}

    def mat(name, ents):
        k = len(M)
        M[name] = ap("WM", ALL, k)
        first = True
        for (r, a, b, s, dr, w) in ents:
            n = len(range(a, b, s))
            if first:
                first = False
                if n == 16:
                    asel(ap("WM", ALL, k), ap("ZE"), [[-16, 8], [-dr, 16]], ALU.not_equal, w, -r, 1)
                    continue
                asel(ap("WM", ALL, k), ap("ZE"), [[-16, 8], [1000, 16]], ALU.not_equal, w, -r - 1000 * a, 1)
                a, r, n = a + s, r + dr, n - 1
                if n == 0:
                    continue
            o = ap("WM", ALL, k, ALL, sl(a, b, s))
            asel(o, o, [[-16, 8], [-dr, n]], ALU.not_equal, w, -r, 1)

    def ident(name, w):
        mat(name, [(0, 0, 16, 1, 1, w)])

    ident("I", 1.0)
    chain("g")
    I = M["I"]
    ts(ap("IT2"), ap("IT"), 15, None, ALU.bitwise_and)
    ts(ap("RO"), ap("IT2"), 0.0, None, ALU.is_equal)
    ts(c("I4", 0, 4), c("IT", 0, 4), 3, None, ALU.bitwise_and)
    ts(ap("IH"), c("I4", 0, 4), 0.0, None, ALU.is_equal)
    BG = c("BO", 0, 128, 16)
    aff(c("CO", 31, 32), c("TS", 0, 1))
    ms(ap("WB0"), 0.0)
    for tb, row in ((1, 0), (1, 1), (2, 3), (2, 4), (3, 6), (3, 7), (1, 11)):
        aff(c("WB0", row + 1, 129, 16), c("TS", 8 * tb, 8 * tb + 8))
    aff(c("WB0", 10, 129, 16), c("ON", 0, 8), c("CO", 31, 32))
    aff(c("WB0", 144 + 13, 272, 16), c("TS", 24, 32))
    aff(c("WB0", 144 + 14, 272, 16), c("ON", 0, 8), c("CO", 31, 32))
    for s in range(4):
        aff(ap("WS", ALL, s), ap("WB0"), c("IH", s, s + 1))
    aff(ap("WB1"), ap("WB0"))
    aff(c("WB1", 12, 129, 16), c("ON", 0, 8), c("CO", 31, 32))
    for s in range(4):
        aff(ap("WS", ALL, 4 + s), ap("WB1"), c("IH", s, s + 1))
    ms(ap("S15"), 0.0)
    for k, w in enumerate((1.0 / 16, 1.0, -1.0)):
        aff(ap("S15", ALL, k, sl(15, 128, 16)), BG, w)
    asel(c("CO", 30, 31), c("ZE2", 0, 1), [[0, 1]], ALU.is_ge, 512.0, -32, 1)
    aff(c("CO", 29, 30), c("RO", 15, 16), -3072.0)
    dd = ((3, 1), (5, 1), (0, -1), (2, -1))
    for nm, outs in (("WPM", (((11, 1), (12, 1)), dd, ((6, 1), (8, 1), (11, -1), (12, -1)), ((9, 1), (10, 1)), ((15, 32), (14, -512)), ((13, 64),),
                              ((13, -64), (14, -256)))),
                     ("WPL", (((0, 1), (2, 1), (14, -512)), dd, ((9, 1), (10, 1)), ((9, 0),), ((14, 64),), ((15, 32),), ((13, -64),)))):
        for o, ents in enumerate(outs):
            for k, (r, w) in enumerate(ents):
                x = c(nm, 8 * o, 8 * o + 8)
                asel(x, x if k else ap("ZE", ALL, 0, sl(0, 8)), [[-16, 8]], ALU.not_equal, w, -r, 1)
    for o, w in enumerate((-1.0, 1.0, 0.0, -1.0)):
        aff(c("WBB", 8 * o, 8 * o + 8), BG, w)
    fill(c("TS", 64, 96), 0.0)
    fill(c("TS", 96, 128), 1.0)
    for ih in range(4):
        aff(ap("SX", ALL, ih), ap("TS"), c("IH", ih, ih + 1), 0.0, "v")
    for h in range(2):
        ms(ap("VT%d" % h, ALL, sl(0, 164 - 32 * h)), 0.0)
        fill(c("TH%d" % h, 0, 32), 63.75)
        fill(c("TH%d" % h, 64, 96), 64.5)

    def atab(a, b, bank):
        aff(c("TT", a, b), c("KO", 128 + a, 128 + b), 1.0, 3064.5)
        mm([(c(bank, 0, b - a), I, c("TT", a, b)), (c(bank, 0, b - a), I, c("KO", 128 + a, 128 + b))])
        aff(c("A", a, b), c(bank, 0, b - a), 1.0, -3072.0)

    def digits(src, hl, dg, w):
        ts(c(dg, 0, w), ap(src), 2072.5, None, ALU.add)
        aff(c(dg, 0, w), c(dg, 0, w), 1.0, -2080.0)
        ts(c(hl, 0, w), ap(src), 15, None, ALU.bitwise_and)
        cp(c(dg, w, 2 * w), c(hl, 0, w))
        ts(c(dg, 2 * w, 3 * w), c(dg, 0, w), c("CO", 30, 31), None, ALU.is_ge)

    def pmm(o, k, dg, w):
        return [(o, ap("WS", ALL, k, sl(1, 129)), c(dg, 0, w)), (o, ap("WS", ALL, k, sl(0, 128)), c(dg, w, 2 * w)),
                (o, ap("WS", ALL, k, sl(144, 272)), c(dg, 2 * w, 3 * w))]

    cp(c("OFF", 0, 64), ap("V0"))
    atab(0, 512, "p4")
    digits("CI", "HI", "DI", 128)
    lst = [(c("p5", 0, 512), ap("S15", ALL, 0), c("TT", 0, 512))]
    for s in range(4):
        lst += pmm(c("p5", 128 * s, 128 * s + 128), s, "DI", 128)
    mm(lst)
    aff(c("P", 128, 640), c("p5", 0, 512), 1.0, c("CO", 29, 30))
    for k in range(4):
        aff(c("Q0", 256 * k, 256 * k + 256), c("q0", 256 * k, 256 * k + 256), 33.0, QC)
    atab(512, 1024, "p6")
    atab(1024, 1536, "p7")
    atab(1536, 1792, "p4")
    digits("CL", "HL", "DL", 320)
    for s, bank in enumerate(("p5", "p6", "p7", "p4")):
        a = 512 + 320 * s
        mm([(c(bank, 0, 320), ap("S15", ALL, 0), c("TT", a, a + 320))] + pmm(c(bank, 0, 320), 4 + s, "DL", 320))
        aff(c("P", 128 + a, 448 + a), c(bank, 0, 320), 1.0, c("CO", 29, 30))

    aff(ap("NB"), ap("BO"), -1.0)
    ident("I16", 16.0)
    ident("N16", -16.0)
    asel(ap("UP"), ap("NB"), [[-1, 128]], ALU.is_gt, 0.0, 0, 1)
    asel(ap("US"), ap("UP"), [[-1, 128]], ALU.not_equal, -2048.0, 0, 1)
    iota(ap("SW"), [[1, 128]], 0, 0)
    fill(ap("WP"), 0.0)
    fill(ap("WW"), 0.0)
    aff(c("WP", 15, 143, 16), BG)
    ts(c("W2", 0, 1), c("WT", 0, 1), 256.0, None, ALU.add)
    ts(c("W2", 1, 2), c("W2", 0, 1), 511, None, ALU.bitwise_and)
    ts(c("CO", 28, 29), c("W2", 1, 2), -256.0, None, ALU.add)
    aff(c("WW", 15, 143, 16), BG, c("CO", 28, 29))
    cp(c("CO", 27, 28), c("IT2", 0, 1))
    aff(c("LW", 0, 8), c("SW", 0, 128, 16), 1.0, c("CO", 27, 28))
    aff(c("LW", 8, 16), c("LW", 0, 8), -1.0, -0.5)
    aff(c("LW", 16, 24), c("LW", 0, 8), 1.0, 1.0)
    for k, w in enumerate((1280.0, 1408.0, 0.0)):
        aff(c("LF", 8 * k, 8 * k + 8), c("LW", 0, 8), 1.0, w, "v")
    aff(ap("WH"), ap("WP"), 1.0 / 16, 0.0, "v")
    aff(ap("IF"), I, 1.0, 0.0, "v")
    ts(ap("PN"), c("SW", 0, 16), c("CO", 27, 28), 4096.0, ALU.is_le, ALU.mult)
    iota(ap("XH"), [[16, 8], [0, 16]], 0, 0)
    iota(ap("XL"), [[0, 8], [1, 16]], 0, 0)
    aff(c("CO", 26, 27), c("RO", 2, 3), 128.0)
    aff(ap("XH"), ap("XH"), c("RO", 0, 1), c("CO", 26, 27))
    aff(ap("XL"), ap("XL"), c("RO", 1, 2))
    tt(ap("XC"), ap("XH"), ap("XL"), ALU.add)
    fill(c("q0", 1024, 1152), 0.0)
    fill(c("rc0", 512, 528), 0.0)
    fill(c("rc1", 512, 528), 0.0)
    aff(c("rc1", 0, 512), c("rc0", 0, 512), 1.0, 1.0)
    aff(ap("BT"), ap("BO"), -32.0)
    al = lambda r, w: (r, 0, 16, 1, 0, w)
    mat("N0", [al(15, 32.0)])
    mat("DN", [al(14, 64.0)])
    mat("V", [al(9, 1.0), al(10, 1.0)])
    mat("XV0", [al(0, -1.0), al(1, -1.0), al(2, -14.0)])
    for nm, w in (("I15", 15.0), ("N15", -15.0), ("I32", 32.0), ("N32", -32.0), ("I31", 31.0), ("N31", -31.0),
                  ("I17", 17.0 / 16), ("I33", 33.0 / 16)):
        ident(nm, w)
    mat("PV", [(0, 0, 2, 1, 0, 1.0), (2, 1, 3, 1, 0, 1.0), (0, 3, 5, 1, 0, 1.0), (2, 4, 6, 1, 0, 1.0), (9, 9, 13, 1, 1, 1.0), (14, 13, 15, 1, 0, 1.0)])
    mat("XR0", [(0, 6, 8, 1, 0, 1.0), (2, 6, 8, 1, 0, 14.0), (1, 7, 9, 1, 0, 1.0)])
    mat("PD", [(3, 3, 5, 1, 0, 1.0), (5, 4, 6, 1, 0, 1.0), (0, 3, 5, 1, 0, -1.0), (2, 4, 6, 1, 0, -1.0)])
    mat("PX", [(3, 0, 2, 1, 0, 1.0), (5, 1, 3, 1, 0, 1.0), (3, 3, 5, 1, 0, 1.0), (5, 4, 6, 1, 0, 1.0), (6, 6, 8, 1, 0, 1.0), (8, 7, 9, 1, 0, 1.0), (13, 13, 16, 1, 1, 1.0)])
    mat("XX", [(0, 9, 12, 2, 0, 1.0), (2, 9, 12, 2, 0, 14.0), (1, 10, 13, 2, 0, 1.0)])
    mat("N1", [al(13, 63.0)])
    mat("E", [al(6, 1.0), al(8, 1.0), al(9, -1.0), al(10, -1.0)])
    mat("D", [al(3, 1.0), al(5, 1.0), al(0, -1.0), al(2, -1.0)])
    mat("C0", [al(0, 1.0), al(2, 1.0)])
    mat("NV", [al(9, -1.0), al(10, -1.0)])
    mat("X128", [al(2, 1.0)])
    mat("XVP", [al(0, -1.0), al(1, -1.0), al(2, 1.0)])
    mat("Z1", [(9, 1, 2, 1, 0, 1.0), (10, 1, 2, 1, 0, 1.0)])
    mat("XU", [(0, 4, 8, 3, 0, 1.0), (1, 4, 8, 3, 0, 1.0), (2, 4, 5, 1, 0, 14.0), (2, 7, 8, 1, 0, 16.0)])
    mat("U1", [(0, 1, 2, 1, 0, 1.0), (2, 1, 2, 1, 0, 1.0)])
    mat("ZD", [(9, 1, 2, 1, 0, -1.0), (10, 1, 2, 1, 0, -1.0), (9, 4, 5, 1, 0, 1.0), (10, 4, 5, 1, 0, 1.0)])
    mat("XD", [(0, 4, 5, 1, 0, -1.0), (1, 4, 5, 1, 0, -1.0), (2, 4, 5, 1, 0, -14.0)])
    mat("UX", [(3, 1, 5, 3, 0, 1.0), (5, 1, 5, 3, 0, 1.0), (6, 7, 8, 1, 0, 1.0), (8, 7, 8, 1, 0, 1.0)])
    mat("UD", [(3, 1, 5, 3, 0, -1.0), (5, 1, 5, 3, 0, -1.0)])
    mat("XO", [(0, 1, 5, 3, 0, 1.0), (1, 1, 5, 3, 0, 1.0), (2, 1, 5, 3, 0, 14.0)])
    mat("XV1", [al(0, -1.0), al(1, -1.0), al(2, -15.0)])
    mat("XR1", [(0, 7, 8, 1, 0, 1.0), (2, 7, 8, 1, 0, 15.0), (1, 7, 8, 1, 0, 1.0)])

    def thr(t, h):
        bank = "p%d" % h
        mm([(c(bank, k, 32, 4), c("q%d" % t, 512 * h + k, 512 * h + 512, 4), BG) for k in range(4)])
        aff(c("TH%d" % h, 32, 64), c(bank, 0, 32), 32.0, THN)

    def back(h, col, terms, up=0):
        return [(c("p%d" % (h + up), col, col + 32), ap("VT%d" % h, ALL, sl(32 * tm + 3 - ih, 32 * tm + 35 - ih)), ap("SX", ALL, ih, sl(0, 32)))
                for tm in terms for ih in range(4)]

    def term(h, a, b):
        return ap("VT%d" % h, ALL, sl(32 * a + 3, 32 * b + 3, 4))

    def step(t, k, h, part):
        bank, Fh, TH = "p%d" % h, "F%d" % h, "TH%d" % h
        o = 64 * (5 * t + k) + 32 * h
        nn = 512 if (t, k) == (0, 0) else (1792 if t == 0 else 1920)
        pg = "PL" if (t, k) == (0, 4) else "PG"
        a = 512 * h
        look = k == 4
        if part == 1 and look:
            ts(term(h, 2, 3), c(bank, 192, 224), 0.5, None, ALU.is_ge)
            chain("v")
        if part == 1 and not look:
            tt(c(Fh, 32, 96), c(bank, 128, 192), c(TH, 32, 96), ALU.is_ge)
            chain("v")
            tt(c(Fh, 32, 64), c(Fh, 32, 64), c(Fh, 64, 96), ALU.is_gt)
            tt(term(h, 0, 3), c(bank, 0, 96), c(Fh, 0, 96), ALU.mult)
            chain("v")
            mm(back(h, 448, (0, 1, 2), 2))
            chain("p")
            if t == 0:
                d = 128 * h + k
                ge(c("DN", d, 128 * h + 128, 4), c(bank, 192, 224), -64.5 if k else -9999.0)
                tt(c("DV", d, 128 * h + 128, 4), c(bank, 96, 128), c("DN", d, 128 * h + 128, 4), ALU.mult)
        if part == 3 and not look:
            cp(c("OFF", o + 64, o + 96), c("p%d" % (h + 2), 448, 480))
            chain("v")
        if part in (1, 3):
            return
        if part == 0:
            act(c(pg, a, a + 512), ind(c("P", 128, 128 + nn), c("OFF", o, o + 32)), AF.Copy)
            chain("s")
        j = part // 2
        b = a + 256 * j
        tt(c("R", b, b + 256), ind(c("A", 0, nn), c("OFF", o + 16 * j, o + 16 * j + 16)), c("Q%d" % t, b, b + 256), ALU.subtract)
        chain("v")
        if part == 0:
            act(c("B", a, a + 256), c("R", a, a + 256), AF.Sign, bias=-3048.0)
            chain("s")
            return
        if TV < 256:
            act(c("B", a + 256, a + 512 - TV), c("R", a + 256, a + 512 - TV), AF.Sign, bias=-3048.0)
            chain("s")
        if TV > 0:
            ts(c("B", a + 512 - TV, a + 512), c("R", a + 512 - TV, a + 512), 3048.0, 0.5, ALU.is_ge, ALU.subtract)
            chain("v")
        ch = lambda nm, j: c(nm, a + j, a + 512, 4)
        mm([(c(bank, j, 224, 4), ch(pg, j), ap("WPL" if look else "WPM")) for j in range(4)], True, False)
        chain("p")
        n0 = 160 if look else 128
        mm([(c(bank, n0 + j, n0 + 32, 4), ch("R", j), c("WBB", 0, 8)) for j in range(4)], False, False)
        if look:
            mm([(c(bank, 128 + j, 224, 4), ch("B", j), c("WBB", 8, 32)) for j in range(4)], False, True)
            return
        mm([(c(bank, 160 + j, 224, 4), ch("B", j), c("WBB", 0, 16)) for j in range(4)], False, True)

    def look_rest(t, h):
        bank, Fh, TH = "p%d" % h, "F%d" % h, "TH%d" % h
        tt(c(Fh, 32, 96), c(bank, 128, 192), c(TH, 0, 64), ALU.is_ge)
        tt(c(Fh, 64, 96), c(Fh, 32, 64), c(Fh, 64, 96), ALU.mult)
        tt(term(h, 0, 2), c(bank, 0, 64), c(Fh, 32, 96), ALU.mult)
        if t == 0:
            a = 128 * h
            aff(c("ND", a, a + 128), c("DN", a, a + 128), -1.0, 1.0)
            scan(c("FS", a, a + 128), c("ND", a, a + 128), c("DV", a, a + 128))
            tt(c("FD", 32 * h, 32 * h + 32), c(bank, 64, 96), c("FS", a + 3, a + 128, 4), ALU.subtract)
            tt(term(h, 3, 4), c("FD", 32 * h, 32 * h + 32), c(Fh, 32, 64), ALU.mult)
            if h == 0:
                cp(term(h, 4, 5), c("FS", 3, 128, 4))
        mm(back(h, 256, (0, 1)))
        o = 64 * t + 32 * h
        ts(c("PX", o, o + 32), c(bank, 256, 288), 512.0, None, ALU.add)
        if t == 0:
            mm(back(h, 288, (3,)))
            cp(c("VB", 32 * h, 32 * h + 32), c("OFF", 256 + 32 * h, 288 + 32 * h))
            tt(c("VB", 32 * h, 32 * h + 32), c("VB", 32 * h, 32 * h + 32), c(bank, 288, 320), ALU.subtract)
            if h == 0:
                mm(back(h, 320, (4,)))
                cp(c("PF", 0, 8), c(bank, 320, 328))
                cp(c("TG", 8, 16), c(bank, 320, 328))
        a = 512 * h
        for j in range(2):
            b = a + 256 * j
            tt(c("X", b, b + 256), ind(c("rc%d" % t, 0, 528), c("PX", o + 16 * j, o + 16 * j + 16)), c("q%d" % t, b, b + 256), ALU.add)
        ge(c("GE", a, a + 512), c("X", a, a + 512), 15.5)
        mm([(c(bank, 0, 512), I, c("X", a, a + 512)), (c(bank, 0, 512), M["N16"], c("GE", a, a + 512))])
        aff(c("q%d" % (t + 1), a, a + 512), c(bank, 0, 512))

    def send(t):
        for h in range(2):
            mm([(c("p2", 64 * h, 128), ap("VT%d" % h, ALL, sl(67 - ih, 99 - ih)), ap("SX", ALL, ih, sl(0, 128 - 64 * h))) for ih in range(4)],
               h == 0, h == 1)
        aff(ap("OW"), c("p2", 0, 128))
        mm([(c("p3", 0, 32), ap("BO"), c("OW", 32, 64)), (c("p3", 32, 64), ap("BO"), c("OW", 96, 128))])
        lst = [(c("p2", 192, 194), ap("BO"), c("OW", 126, 128))]
        for h in range(2):
            lst += [(c("p2", 128 + 32 * h, 160 + 32 * h), ap("BO"), c("OW", 32 + 64 * h, 64 + 64 * h)),
                    (c("p2", 128 + 32 * h, 160 + 32 * h), ap("UP"), c("OW", 64 * h, 32 + 64 * h))]
        mm(lst)
        for k in range(6):
            act(c("JK", 64 * k, 64 * k + 64), c("p3", 0, 64), AF.Sign, bias=c("LW", 8 + k, 9 + k), acc=c("SG", k, k + 1))
        aff(c("INC", 0, 66), c("p2", 128, 194))
        ts(c("CU", 0, 6), c("SG", 0, 6), -0.5, 32.0, ALU.mult, ALU.add)
        tt(ap("CM"), ind(c("INC", 0, 66), c("CU", 0, 6)), c("SW", 0, 96), ALU.is_le)
        aff(c("CB", 0, 6), c("SG", 0, 6), -0.5, 32.0)
        ts(c("CB", 8, 14), c("LW", 16, 22), c("INC", 65, 66), 0.0, ALU.subtract, ALU.max)
        se = "SE%d" % t
        ts(c(se, 96, 192), c("SW", 0, 96), c("INC", 65, 66), None, ALU.is_ge)
        o = c("p3", 64, 70)
        mm([(o, M["I16"], c("CB", 0, 6)), (o, I, c("CB", 8, 14))] + [(o, c("WP", 15 - i, 143 - i), c("CM", i, 96, 16)) for i in range(16)])
        ln = c("LN", 8 * t, 8 * t + 6)
        cp(ln, o)
        cp(c(se, 0, 96), ind(c("q%d" % t, 0, 1152), ln))
        add([("g", 300, t)], [ap(se)], [], "send")
        if t == 0:
            lst = []
            for h in range(2):
                lst += [(c("p2", 256 + 32 * h, 288 + 32 * h), ap("BO"), c("OW", 32 + 64 * h, 64 + 64 * h)),
                        (c("p2", 256 + 32 * h, 288 + 32 * h), ap("US"), c("OW", 64 * h, 32 + 64 * h))]
            mm(lst)
            ge(c("SL", 0, 64), c("p2", 256, 320), -1951.5, -1.0)
            ge(c("SL", 64, 128), c("p2", 256, 320), -1951.5)

    def recv(t):
        se, rx = "SE%d" % t, "RX%d" % t
        add([("r", 5500, t)], [ap(se)], [ap(rx)], "recv")
        ln = c("LN", 8 * t, 8 * t + 6)
        tt(ap("TQ"), c(rx, 96, 192), c(se, 0, 96), ALU.mult)
        tt(ind(c("q%d" % (t + 1), 0, 1152), ln), ap("TQ"), c(rx, 0, 96), ALU.add)
        if t == 0:
            tt(c("VB", 64, 128), c("VB", 0, 64), c("SL", 64, 128), ALU.mult)
            mm([(c("p2", 320, 384), c("WW", 15 - i, 143 - i), c("q1", i, 1024, 16)) for i in range(16)])
            for k in range(4):
                aff(c("Q1", 256 * k, 256 * k + 256), c("q1", 256 * k, 256 * k + 256), 33.0, QC)
            tt(c("HS", 0, 64), c("p2", 320, 384), c("SL", 0, 64), ALU.mult)
            ts(c("HS", 64, 128), c("HS", 0, 64), 511, None, ALU.bitwise_and)
            tt(c("VB", 0, 64), c("HS", 64, 128), c("VB", 64, 128), ALU.add)
            cp(c("OFF", 320, 384), c("VB", 0, 64))
            thr(1, 0)
            thr(1, 1)
            fill(c("q1", 1024, 1152), 0.0)

    OK, RT, BB = c("bb", 128, 256), c("bb", 256, 384), c("bb", 0, 128)
    XC = ap("XC")

    def wrap(o, plus):
        mm([(o, c("WH", 15 - i, 143 - i), c("tf", i, 128, 16)) for i in range(16)] + ([(o, ap("IF"), plus)] if plus else []))

    def lowest(pg, extra, tg, lw):
        tt(ap("tf"), c("p6", 256, 384), OK, ALU.mult)
        wrap(c("p5", 96, 104), None)
        aff(c("KV", 0, 8), c("p5", 96, 104))
        pos, o, e = [], 0, 0
        for k in range(8):
            w = 128 - 16 * k
            if k == 5:
                o = 0
            pos.append(("p7" if k < 5 else "p5", o, e, w))
            o += w
            e += w
        for bank, o, e, w in pos:
            lst = [(c(bank, o, o + w), M["V"], c(pg[0], pg[1] + 128 - w, pg[1] + 128))]
            if extra:
                lst.append((c(bank, o, o + w), M["X128"], c("XC", 0, w)))
            mm(lst + [(c(bank, o, o + 16), I, ap("PN"))])
        for k, (bank, o, e, w) in enumerate(pos):
            ts(c("ES", e, e + w), c(bank, o, o + w), c("KV", k, k + 1), None, ALU.is_equal)
        mm([(c("p5", 256 - w, 256), ap("BO"), c("ES", e, e + w)) for bank, o, e, w in pos])
        ts(c("p5", 128, 256), c("p5", 128, 256), 0.5, None, ALU.is_lt)
        tt(ap("wn"), c("p5", 128, 256), OK, ALU.mult)
        tt(ap("tf"), c("p6", 384, 512), ap("wn"), ALU.mult)
        wrap(c("p7", 480, 488), lw)
        cp(tg, c("p7", 480, 488))

    KG, T1, T0 = c("kg", 0, 128), c("kg", 128, 256), c("kg", 256, 384)

    def keys(win, off):
        act(KG, ind(win, off), AF.Copy)
        aff(T1, KG, 1.0, 3064.5)
        aff(T0, T1, 1.0, -3072.0)

    def kvals(q, tg, win, x):
        mm([(c("p4", 0, 128), I, q), (c("p4", 0, 128), M["I16"], KG), (c("p4", 0, 128), M["N16"], T0)])
        mm([(c("p4", 128, 256), M["I15"], q), (c("p4", 128, 256), M["N15"], KG), (c("p4", 128, 256), M["I15"], T0)])
        mm([(c("p5", 256, 384), M["I17"], T0)])
        tt(c("vk", 0, 128), c("p4", 128, 256), BB, ALU.mult)
        aff(c("vk", 128, 256), c("p4", 0, 128))
        tt(ind(win, tg), c("vk", 0, 128), c("vk", 128, 256), ALU.add)
        tt(c("KO", 128 + x, 256 + x), c("p5", 256, 384), ap("wn"), ALU.mult)

    def insert(t):
        pgn = "PL" if t == 0 else "PG"
        pg, q, x = c(pgn, 0, 128), c("q%d" % t, 0, 128), 1792 + 128 * t
        keys(c("KO", 128, 128 + x), c("OFF", 64 * (5 * t + 4), 64 * (5 * t + 4) + 8))
        mm([(c("p6", 128, 256), ap("BO"), c("B", 0, 128)), (c("p6", 128, 256), M["DN"], pg)])
        mm([(c("p6", 256, 384), M["V"], pg)])
        mm([(c("p6", 384, 512), M["V"], pg), (c("p6", 384, 512), M["XV%d" % t], XC)])
        mm([(c("p6", 0, 128), ap("NB"), c("R", 0, 128)), (c("p6", 0, 128), M["N0"], pg), (c("p6", 0, 128), ap("BT"), q)])
        ge(OK, c("p6", 128, 256), 63.5)
        ge(BB, c("p6", 0, 128), THN)
        tg = c("TG", 0, 8)
        lowest((pgn, 0), False, tg, c("LF", 8 * t, 8 * t + 8))
        a0, a1, a2 = c("p6", 0, 128), c("p6", 128, 256), c("p6", 256, 384)
        sp, sn = ap("S15", ALL, 1), ap("S15", ALL, 2)
        if t == 0:
            mm([(a0, M["PV"], pg), (a0, M["XR0"], XC), (a0, sp, KG), (a0, sn, T0)])
            mm([(a1, M["PD"], pg), (a1, sp, q), (a1, sn, KG), (a1, sp, T0)])
            mm([(a2, M["PX"], pg), (a2, M["XX"], XC)])
            mm([(c("p4", 256, 384), I, q), (c("p4", 256, 384), M["I32"], KG), (c("p4", 256, 384), M["N32"], T0)])
            mm([(c("p4", 384, 512), M["I31"], q), (c("p4", 384, 512), M["N31"], KG), (c("p4", 384, 512), M["I31"], T0)])
            mm([(c("p5", 384, 512), M["I33"], T0)])
            tt(c("va", 0, 128), c("p4", 384, 512), BB, ALU.mult)
            aff(c("va", 128, 256), c("p4", 256, 384))
            tt(ind(c("A", 512, 1920), tg), c("va", 0, 128), c("va", 128, 256), ALU.add)
            aff(c("A", 1792, 1920), c("p5", 384, 512))
        else:
            mm([(a0, M["PV"], pg), (a0, M["XR1"], XC)])
            mm([(a1, M["PD"], pg)])
            mm([(a2, M["PX"], pg)])
        tt(c("vp", 0, 128), a1, BB, ALU.mult)
        aff(c("vp", 128, 256), a0)
        tt(ind(c("P", 640, 256 + x), tg), c("vp", 0, 128), c("vp", 128, 256), ALU.add)
        tt(c("P", 128 + x, 256 + x), a2, ap("wn"), ALU.mult)
        kvals(q, tg, c("KO", 640, 256 + x), x)
        if t == 0:
            aff(ap("NP"), ap("wn"), -4096.0, 4096.0)

    def post():
        pz, mb = c("PL", 0, 128), c("mz", 128, 256)
        act(c("mz", 0, 128), ind(c("KO", 128, 2048), c("OFF", 256, 264)), AF.Copy)
        aff(c("mz", 0, 128), c("mz", 0, 128), 1.0, 3064.5)
        aff(ap("MQ"), c("mz", 0, 128), 33.0 / 16, QC - 6336.0)
        aff(mb, c("mz", 0, 128), 1.0 / 16, -192.0)
        rr, bb, pg = c("Re", 0, 128), c("Re", 128, 256), c("Re", 256, 384)
        oe, ou = c("TG", 8, 16), c("TG", 16, 24)
        act(pg, ind(c("P", 128, 640), oe), AF.Copy)
        tt(rr, ind(c("A", 0, 512), oe), ap("MQ"), ALU.subtract)
        ts(bb, rr, 3048.0, 0.5, ALU.is_ge, ALU.subtract)
        mm([(c("p6", 0, 128), ap("NB"), bb), (c("p6", 0, 128), M["N1"], pg)])
        mm([(c("p6", 128, 256), M["E"], pg)])
        ge(RT, c("p6", 0, 128), 63.5)
        tt(ap("tf"), c("p6", 128, 256), RT, ALU.mult)
        wrap(c("p7", 480, 488), c("PF", 0, 8))
        cp(ou, c("p7", 480, 488))
        act(pg, ind(c("P", 128, 640), ou), AF.Copy)
        tt(rr, ind(c("A", 0, 512), ou), ap("MQ"), ALU.subtract)
        keys(c("KO", 128, 640), ou)
        mm([(c("p6", 0, 128), ap("NB"), rr), (c("p6", 0, 128), M["N0"], pg), (c("p6", 0, 128), ap("BT"), mb)])
        mm([(c("p4", 0, 128), M["D"], pg)])
        mm([(c("p4", 128, 256), M["C0"], pg), (c("p4", 128, 256), M["NV"], pz)])
        mm([(c("p6", 256, 384), M["V"], pg), (c("p6", 256, 384), M["X128"], XC)])
        mm([(c("p6", 384, 512), M["V"], pg), (c("p6", 384, 512), M["XVP"], XC)])
        ge(BB, c("p6", 0, 128), THN)
        tt(ap("t1"), c("p4", 0, 128), BB, ALU.mult)
        tt(c("p6", 128, 256), c("p4", 128, 256), ap("t1"), ALU.add)
        tt(OK, c("p6", 128, 256), ap("NP"), ALU.is_equal)
        tg = c("TG", 24, 32)
        lowest(("Re", 256), True, tg, c("LF", 16, 24))
        a0, a1, a2, a3 = [c("p6", 128 * k, 128 * k + 128) for k in range(4)]
        mm([(a0, M["Z1"], pz), (a0, M["XU"], XC)])
        mm([(a1, M["U1"], pg), (a1, M["ZD"], pz), (a1, M["XD"], XC)])
        mm([(a2, M["UX"], pg)])
        mm([(a3, M["UD"], pg), (a3, M["XO"], XC)])
        tt(c("vq", 0, 128), a1, BB, ALU.mult)
        aff(c("vq", 128, 256), a0)
        tt(ap("t1"), a3, BB, ALU.mult)
        tt(c("p7", 0, 128), a2, ap("t1"), ALU.add)
        tt(c("P", 2176, 2304), c("p7", 0, 128), ap("wn"), ALU.mult)
        kvals(mb, tg, c("KO", 0, 640), 2048)
        dma("y", c("yk", 0, 512), c("KO", 128, 640), 131072)
        dma("y", c("yk", 2048, 2176), c("KO", 2176, 2304), 32768)

    thr(0, 0)
    thr(0, 1)
    for t in range(2):
        for s in range(11):
            for part in range(4):
                u = s - part % 2
                if 0 <= u < 10:
                    step(t, u // 2, u % 2, part)
        send(t)
        if t == 1:
            tt(ind(c("P", 0, 640), c("TG", 24, 32)), c("vq", 0, 128), c("vq", 128, 256), ALU.add)
        insert(t)
        look_rest(t, 0)
        look_rest(t, 1)
        recv(t)
        if t == 0:
            post()
    dma("y", c("yk", 512, 1280), c("KO", 640, 1408), 200000)
    dma("s", c("yk", 1280, 2048), c("KO", 1408, 2176), 200000)
    for nm, row in (("y0", 1), ("y1", 4), ("yr", 7)):
        dma("y", ap(nm), ap("P", sl(row, 128, 16), sl(128, 2304)), 70000)
    dma("y", c("yq", 0, 512), c("q2", 0, 512), 131072)
    dma("s", c("yq", 512, 1024), c("q2", 512, 1024), 131072)
    return ops


def schedule(ops):
    acc = {}
    lastp = {}
    n = len(ops)
    for i, o in enumerate(ops):
        dep = {}
        for mode, lst in (("r", o["rd"]), ("w", o["wr"])):
            for (nm, p0, p1, c0, c1, st) in sorted(set(lst)):
                if SCRATCH[nm][0] == "psum" and lastp.get(nm, i) != i:
                    dep[lastp[nm]] = max(dep.get(lastp[nm], 0), 1)
                for (j, m, q0, q1, d0, d1, su) in acc.get(nm, []):
                    if p0 < q1 and q0 < p1 and c0 < d1 and d0 < c1 and not (st == su and (c0 - d0) % st):
                        if m == "w":
                            dep[j] = 2
                        elif mode == "w":
                            dep[j] = max(dep.get(j, 0), 1)
        for mode, lst in (("r", o["rd"]), ("w", o["wr"])):
            for (nm, p0, p1, c0, c1, st) in sorted(set(lst)):
                acc.setdefault(nm, []).append((i, mode, p0, p1, c0, c1, st))
                if SCRATCH[nm][0] == "psum":
                    lastp[nm] = i
        if "after" in o:
            dep[o["after"]] = max(dep.get(o["after"], 0), 1)
        o["dep"] = dep
    sends = {}
    for i, o in enumerate(ops):
        if o["kind"] == "send":
            sends[o["alts"][0][2]] = i
        if o["kind"] == "recv":
            o["dep"] = {sends[o["alts"][0][2]]: 2}
    dur = [o["alts"][0][1] + (o["x"][1] if o["kind"] == "d" else 0) for o in ops]
    prio = [0.0] * n
    succ = [[] for _ in range(n)]
    for i, o in enumerate(ops):
        for j in o["dep"]:
            succ[j].append(i)
    for i in range(n - 1, -1, -1):
        prio[i] = dur[i] + max([prio[j] + 80 for j in succ[i]] + [0.0])
    best = None
    for it in range(ITER):
        got = place(ops, succ, prio)
        order, eng, start, fin = got
        if best is None or max(fin) < max(best[3]):
            best = got
        before, lastq = {}, {}
        for (i, e, f) in order:
            before[i] = lastq.get(e)
            lastq[e] = i
        i = max(range(n), key=lambda j: fin[j])
        while i is not None:
            prio[i] += STEP
            j = max(list(ops[i]["dep"]) + [-1], key=lambda d: fin[d] if d >= 0 else -1.0)
            k = before[i] if eng[i] != "r" else None
            if k is not None and ops[k]["kind"] == "c" and fin[k] > start[i] - 5 and k not in ops[i]["dep"]:
                prio[k] -= 2 * STEP
                i = k
            else:
                i = j if j >= 0 else None
    return best


def place(ops, succ, prio):
    n = len(ops)
    left = [len(o["dep"]) for o in ops]
    free = {e: 0.0 for e in "vspgyr"}
    fin, eng, start = [None] * n, [None] * n, [0.0] * n
    avail = [i for i in range(n) if left[i] == 0]
    order = []

    def ready(i, e):
        r = 0.0
        for j, k in ops[i]["dep"].items():
            if eng[j] == e and ops[j]["kind"] == "c" and (k == 1 or e == "p"):
                r = max(r, start[j])
            else:
                r = max(r, fin[j] + (60 if eng[j] == e else 110))
        return r

    rd = {}
    while avail:
        cand = []
        for i in avail:
            for (e, cost, f) in ops[i]["alts"]:
                if (i, e) not in rd:
                    rd[i, e] = ready(i, e) + (SLACK if e == "v" and len(ops[i]["alts"]) > 1 else 0)
                cand.append((max(free[e], rd[i, e]), i, e, cost, f))
        t0 = min(x[0] for x in cand)
        e0 = min(cand, key=lambda x: (x[0], -prio[x[1]]))[2]
        near = [x for x in cand if x[2] == e0 and x[0] <= t0 + LOOK]
        s, i, e, cost, f = max(near, key=lambda x: prio[x[1]])
        if e != "p":
            hot = [x for x in cand if x[2] == "p" and x[0] + x[3] + 110 < s + cost - TOL and
                   any(left[y] == 1 and ops[y]["alts"][0][0] == e and prio[y] > prio[i] + MARG for y in succ[x[1]])]
            if hot:
                s, i, e, cost, f = max(hot, key=lambda x: prio[x[1]])
        urgent = [x for x in cand if x[2] == e and prio[x[1]] > prio[i] + MARG and x[0] < s + cost - TOL]
        if urgent:
            u = min(urgent, key=lambda x: x[0])
            fit = [x for x in cand if x[2] == e and x[0] + x[3] <= u[0] + TOL]
            s, i, e, cost, f = max(fit, key=lambda x: prio[x[1]]) if fit else u
        if e == "v" and len(ops[i]["alts"]) > 1:
            s = max(free[e], rd[i, e] - SLACK)
        eng[i], start[i] = e, s
        free[e] = s + cost if e != "r" else 0.0
        fin[i] = s + cost + (ops[i]["x"][1] if ops[i]["kind"] == "d" else 0)
        order.append((i, e, f))
        avail.remove(i)
        for j in succ[i]:
            left[j] -= 1
            if left[j] == 0:
                avail.append(j)
    return order, eng, start, fin


_PLAN = []


def plan():
    if not _PLAN:
        ops = program()
        _PLAN.append((ops, schedule(ops)))
    return _PLAN[0]


def relay_of(src, dst, topo):
    ok = [k for k in topo.cores_of(src) if k != src and topo.may_write(k, dst)]
    same = [k for k in ok if topo.die(k) == topo.die(src)]
    return (same or ok)[0]


def first_engines(src, dst, n, topo):
    m = 0
    for e in topo.engines(src, dst)[:n]:
        m |= 1 << e
    return m


def rank_program(g, core, T, topo):
    cores = list(T.cores)
    N = len(cores)
    S = T.sem
    rank = T.rank_of(core)
    if rank is None:
        for a in range(N):
            src, dst = cores[a], cores[(a + 1) % N]
            if not topo.may_write(src, dst) and relay_of(src, dst, topo) == core:
                rid, pid = topo.addr(dst, core)
                for t in range(2):
                    g.wait_ge(S["ra%d" % t], NE)
                    g.remote_dma(T["RX%d" % t][:], T["RB%d" % t][:], S["rx%d" % t], S.lr, pid, rid, first_engines(core, dst, NE, topo))
                g.wait_ge(S.lr, 2 * NE)
        return
    ops, (order, eng, start, fin) = plan()
    Q = {"v": g.vector, "s": g.scalar, "p": g.tensor, "g": g, "y": g.sync}
    SEM = {"v": "sv", "s": "ss", "p": "sp", "g": "sg"}
    cnt = {k: 0 for k in SEM.values()}
    known = {e: {} for e in Q}
    sig = {}
    dst = cores[(rank + 1) % N]
    direct = topo.may_write(core, dst)
    hop = dst if direct else relay_of(core, dst, topo)
    rid, pid = topo.addr(hop, core)
    for (i, e, f) in order:
        o = ops[i]
        if o["kind"] == "recv":
            sig[i] = ("rx%d" % f, NE)
            continue
        need = {}
        for j, k in o["dep"].items():
            if eng[j] == e and ops[j]["kind"] == "c" and (k == 1 or e == "p"):
                continue
            s, v = sig[j]
            need[s] = max(need.get(s, 0), v)
        for s, v in need.items():
            if known[e].get(s, 0) < v:
                Q[e].wait_ge(S[s], v)
                known[e][s] = v
        if o["kind"] == "send":
            g.remote_dma(T[("RX%d" if direct else "RB%d") % f][:], T["SE%d" % f][:], S[("rx%d" if direct else "ra%d") % f], S.ls, pid, rid,
                         first_engines(core, hop, NE, topo))
            sig[i] = ("ls", NE * (f + 1))
        elif o["kind"] == "d":
            f(Q[e], T).then_inc(S[o["x"][0]], 16)
            sig[i] = (o["x"][0], 16)
        else:
            f(Q[e], T).then_inc(S[SEM[e]], 1)
            cnt[SEM[e]] += 1
            sig[i] = (SEM[e], cnt[SEM[e]])
    last = {}
    for s, v in sig.values():
        last[s] = max(last.get(s, 0), v)
    for s, v in last.items():
        g.wait_ge(S[s], v)
